import numpy as np
import ml_dtypes


def mxq(x, axis, fmt="e4m3"):
    dtype, down = {"e4m3": (ml_dtypes.float8_e4m3fn, 7), "e5m2": (ml_dtypes.float8_e5m2, 14)}[fmt]
    v = np.moveaxis(np.asarray(x, np.float32).astype(ml_dtypes.bfloat16).astype(np.float64), axis, -1)
    blocks = v.reshape(v.shape[:-1] + (-1, 32))
    amax = np.abs(blocks).max(-1, keepdims=True)
    byte = np.maximum(np.where(amax > 0, np.frexp(amax)[1] - 1 + 127, 0) - down, 1)
    scale = np.exp2(byte - 127.0)
    codes = (blocks / scale).astype(np.float32).astype(dtype).astype(np.float64)
    return np.moveaxis((codes * scale).reshape(v.shape), -1, axis)


WIDE = False


def mx_kscale(k):
    if not WIDE:
        return np.ones(k)
    levels = np.array([10, -10, 5, -5, 0])
    if k % 512:
        return np.exp2(np.random.permutation(np.resize(levels, k // 32))).repeat(32)
    a = np.empty((k // 512, 16))
    for p in range(k // 512):
        a[p, :8] = np.random.permutation(np.resize(levels, 8))
        for g in range(8):
            far = levels[np.abs(levels - a[p, g]) >= 10]
            a[p, g + 8] = far[np.random.randint(len(far))]
    return np.exp2(a.ravel()).repeat(32)


def f64(x):
    return np.asarray(x).astype(np.float64)


def striped(idx):
    return np.tile(idx.reshape(-1, 16).T, (8, 1)).astype(np.uint16)


def unstriped(offs):
    return offs[:16].T.reshape(-1).astype(np.int64)


def striped8(idx):
    return np.concatenate([x.reshape(-1, 16).T for x in idx]).astype(np.uint16)


def runs(offs, k):
    lists = np.stack([offs[16 * r : 16 * r + 16].T.reshape(-1) for r in range(8)]).astype(np.int64)
    return lists[np.arange(k) % 512 // 64]


def pack_weight(w):
    k, n = w.shape
    w = f64(np.asarray(w, np.float32).astype(ml_dtypes.bfloat16)).reshape(k // 32, 32, n)
    amax = np.abs(w).max(1)
    byte = np.clip(np.where(amax > 0, np.frexp(amax)[1] - 1 + 127 - 7, 1), 1, 254)
    scaled = (w * np.exp2(127.0 - byte)[:, None, :]).reshape(k, n).astype(np.float32)
    words = np.ascontiguousarray(scaled.reshape(k // 512, 128, 4, n).transpose(0, 1, 3, 2)).astype(ml_dtypes.float8_e4m3fn).view(np.uint8)
    return words, np.ascontiguousarray(byte.astype(np.uint8).reshape(k // 512, 16, n))


def unpack_weight(words, scales):
    g, p, n, _ = words.shape
    vals = np.ascontiguousarray(words).view(ml_dtypes.float8_e4m3fn).astype(np.float64) * np.repeat(np.exp2(scales.astype(np.float64) - 127.0), 8, axis=1)[..., None]
    return vals.transpose(0, 1, 3, 2).reshape(g * 512, n)


K, T, S, H, C = 512, 2048, 512, 512, 512


def setup_inputs():
    n = np.random.standard_normal
    s = mx_kscale(K)[:, None]
    packed_xT = pack_weight(n((K, T)) * s)
    return {
        "x_words": packed_xT[0],
        "x_scales": packed_xT[1],
        "w1": (n((K, H)) / np.sqrt(K) / s).astype(np.float32),
        "gs": (np.random.uniform(0.5, 1.5, (K, 1)) / s).astype(np.float32),
        "offs": striped(np.random.permutation(T)[:S]),
        "q0": striped8(np.stack([np.random.permutation(S) for _ in range(8)])),
        "q1": striped8(np.stack([np.random.permutation(S) for _ in range(8)])),
        "q2": striped8(np.stack([np.random.permutation(S) for _ in range(8)])),
        "q3": striped8(np.stack([np.random.permutation(S) for _ in range(8)])),
        "cand": striped(np.random.permutation(T)[:C]),
    }


def reference(x_words, x_scales, w1, gs, offs, q0, q1, q2, q3, cand):
    x_cand = unpack_weight(x_words, x_scales)[:, unstriped(cand)]
    xq = unpack_weight(x_words, x_scales)[:, unstriped(offs)]
    y = mxq(f64(w1), 0, "e4m3").T @ xq
    a = y[np.arange(H)[:, None], runs(q0, H)]
    c = y[np.arange(H)[:, None], runs(q2, H)]
    b = y[np.arange(H)[:, None], runs(q1, H)]
    d = y[np.arange(H)[:, None], runs(q3, H)]
    z = f64(gs) * (((a - c) * (b - d)) / ((a - d) ** 2 + (b - c) ** 2 + 0.5))
    return 0.0625 * ((x_cand.T @ mxq(z, 0, "e4m3")))

@@ -1,0 +1,226 @@
+from contextlib import ExitStack
+
+import concourse.mybir as mybir
+from concourse.masks import make_identity
+
+K, T, S, H, C = 512, 2048, 512, 512, 512
+FLOPS = 2 * K * H * S + 2 * K * C * S
+
+F32 = mybir.dt.float32
+BF16 = mybir.dt.bfloat16
+I32 = mybir.dt.int32
+U32 = mybir.dt.uint32
+U16 = mybir.dt.uint16
+U8 = mybir.dt.uint8
+FP8X4 = mybir.dt.float8_e4m3fn_x4
+ALU = mybir.AluOpType
+ACT = mybir.ActivationFunctionType
+
+P = 128
+PACK = 4
+CH = 128
+GROUPS = [(0, 256), (256, 128), (384, 128)]
+W_LOADS = [(0, 256), (256, 256)]
+
+
+def tile_picked_crossrat_none_p_kernel(
+    tc, x_words, x_scales, w1, gs, offs, q0, q1, q2, q3, cand, out
+):
+    nc = tc.nc
+    with ExitStack() as ctx:
+        keep = ctx.enter_context(tc.tile_pool(name="keep", bufs=1))
+        work = ctx.enter_context(tc.tile_pool(name="work", bufs=2))
+        psum = ctx.enter_context(tc.psum_pool(name="psum", bufs=1))
+
+        def load_list(src, name):
+            lst = keep.tile([P, S // 16], U16, name=name)
+            nc.sync.dma_start(lst[:], src)
+            return lst
+
+        x_bytes = keep.tile([P, T], U8)
+        nc.vector.memset(x_bytes[:].bitcast(I32), 0)
+
+        four = keep.tile([P, 1], F32)
+        nc.gpsimd.memset(four[:], 4.0)
+        warm = keep.tile([P, 1], F32)
+        nc.scalar.activation(warm[:], four[:], ACT.Abs_reciprocal_sqrt)
+
+        staged = keep.tile([P, T], U8)
+        for q in range(4):
+            nc.sync.dma_start(
+                staged[32 * q : 32 * q + 4, :].bitcast(I32), x_scales[0, 4 * q : 4 * q + 4, :].bitcast(I32)
+            )
+        offs_sb = load_list(offs, "offs_sb")
+        cand_sb = load_list(cand, "cand_sb")
+        w_rows = w1.rearrange("(p j) c -> p j c", j=PACK)
+        w_raw = []
+        for n, (c0, cw) in enumerate(W_LOADS):
+            raw = keep.tile([P, PACK, cw], F32, name=f"w_raw{n}")
+            nc.sync.dma_start(raw[:], w_rows[:, :, c0 : c0 + cw])
+            w_raw.append(raw[:])
+        x_packed = keep.tile([P, T], I32)
+        nc.sync.dma_start(x_packed[:], x_words[0].rearrange("p n r -> p (n r)").bitcast(I32))
+        q3_sb = load_list(q3, "q3_sb")
+        q0_sb = load_list(q0, "q0_sb")
+        q1_sb = load_list(q1, "q1_sb")
+        q2_sb = load_list(q2, "q2_sb")
+        for q in range(4):
+            rows = slice(32 * q, 32 * q + 4)
+            nc.vector.tensor_copy(x_bytes[rows, :].bitcast(I32), staged[rows, :].bitcast(I32))
+        gs_sb = keep.tile([P, PACK], F32)
+        nc.sync.dma_start(gs_sb[:], gs.rearrange("(p t) o -> p (t o)", t=PACK))
+
+        ident = keep.tile([P, P], F32)
+        make_identity(nc, ident[:])
+
+        def pick_scales(lst, name):
+            scales = keep.tile([P, S], U8, name=name, align_bytes=64)
+            nc.vector.tensor_copy(scales[:], x_bytes[:].indirect(lst[:]))
+            return scales
+
+        def pick_codes(lst, name):
+            codes = keep.tile([P, S], U32, name=name, align_bytes=64)
+            nc.vector.tensor_copy(codes[:], x_packed[:].bitcast(U32).indirect(lst[:]))
+            return codes
+
+        xq_scales = pick_scales(offs_sb, "xq_scales")
+        xc_scales = pick_scales(cand_sb, "xc_scales")
+
+        w_half = [keep.tile([P, PACK, 64, PACK], BF16, name=f"w_half{h}", tag=f"w_half{h}", align_bytes=64) for h in range(2)]
+        w_codes = keep.tile([P, PACK, P], U32, align_bytes=64)
+        w_scales = keep.tile([P, PACK, P], U8, align_bytes=64)
+        for n, (c0, cw) in enumerate(W_LOADS):
+            h, m0 = divmod(c0 // PACK, 64)
+            dst = w_half[h][:, :, m0 : m0 + cw // PACK, :].rearrange("p t m j -> p m j t")
+            src = w_raw[n].rearrange("p j (m t) -> p m j t", t=PACK)
+            nc.scalar.copy(dst, src)
+        for h in range(2):
+            for t in range(PACK):
+                nc.vector.quantize_mx(
+                    out=w_codes[:, t, 64 * h : 64 * h + 64].bitcast(FP8X4),
+                    scales=w_scales[:, t, 64 * h : 64 * h + 64],
+                    in_=w_half[h][:, t, :, :].rearrange("p m j -> p (m j)"),
+                )
+
+        xq_codes = keep.tile([P, S], U32, align_bytes=64)
+        for h in range(2):
+            nc.vector.tensor_copy(
+                xq_codes[:, 256 * h : 256 * h + 256], x_packed[:].bitcast(U32).indirect(offs_sb[:, 16 * h : 16 * h + 16])
+            )
+        xc_codes = pick_codes(cand_sb, "xc_codes")
+
+        y, y_neg = [], []
+        for t in range(PACK):
+            pos = keep.tile([P, S], F32, name=f"y{t}")
+            neg = keep.tile([P, S], F32, name=f"y_neg{t}")
+            pieces = [slice(0, 256), slice(256, 512)] if t == 0 else [slice(0, 512)]
+            accs = []
+            for n, cols in enumerate(pieces):
+                if n == 0:
+                    acc = psum.tile([P, cols.stop - cols.start], F32, name=f"y_acc{t}", tag=f"bank{t}")
+                else:
+                    acc = psum.tile([P, cols.stop - cols.start], F32, name="y_late", tag="unit", bufs=4)
+                nc.tensor.matmul_mx(
+                    out=acc[:],
+                    lhsT=w_codes[:, t, :].bitcast(FP8X4),
+                    lhsT_scale=w_scales[:, t, :],
+                    rhs=xq_codes[:, cols].bitcast(FP8X4),
+                    rhs_scale=xq_scales[:, cols],
+                    start=True,
+                    stop=True,
+                )
+                nc.scalar.copy(pos[:, cols], acc[:])
+                accs.append(acc)
+            for acc, cols in zip(accs, pieces):
+                nc.scalar.mul(neg[:, cols], acc[:], -1.0)
+            y.append(pos)
+            y_neg.append(neg)
+
+        def turn(bank, t, *terms):
+            for n, term in enumerate(terms):
+                nc.tensor.matmul(
+                    bank[:, t, :], term, ident[:], start=(n == 0), stop=(n == len(terms) - 1), is_transpose=True
+                )
+
+        diffs = {}
+
+        def gather(j0, width):
+            cols = slice(j0 // 16, (j0 + width) // 16)
+            d = keep.tile([P, PACK, width], F32, name=f"d{j0}")
+            ad = keep.tile([P, PACK, width], F32, name=f"ad{j0}")
+            bd = keep.tile([P, PACK, width], F32, name=f"bd{j0}")
+            dc = keep.tile([P, PACK, width], F32, name=f"dc{j0}")
+            nc.vector.tensor_copy(d[:, 0, :], y[0][:].indirect(q3_sb[:, cols]))
+            for t in range(PACK):
+                if t + 1 < PACK:
+                    nc.vector.tensor_copy(d[:, t + 1, :], y[t + 1][:].indirect(q3_sb[:, cols]))
+                nc.vector.tensor_tensor(ad[:, t, :], y[t][:].indirect(q0_sb[:, cols]), d[:, t, :], ALU.subtract)
+                nc.vector.tensor_tensor(bd[:, t, :], y[t][:].indirect(q1_sb[:, cols]), d[:, t, :], ALU.subtract)
+                nc.vector.tensor_tensor(dc[:, t, :], y_neg[t][:].indirect(q2_sb[:, cols]), d[:, t, :], ALU.add)
+            for j in range(0, width, CH):
+                diffs[(j0 + j) // CH] = [x[:, :, j : j + CH] for x in (ad, bd, dc)]
+
+        parts = {}
+
+        def sums(c, t):
+            ad, bd, dc = diffs[c]
+            if t == 0:
+                ac = psum.tile([P, PACK, CH], F32, name=f"ac{c}", tag=f"bank{c}")
+                inv = keep.tile([P, PACK, CH], F32, name=f"inv{c}")
+                parts[c] = (ac, bd, inv)
+            ac, bd, inv = parts[c]
+            unit = psum.tile([P, 4, CH], F32, name="unit", tag="unit", bufs=4)
+            turn(unit, 0, ad[:, t, :])
+            turn(unit, 1, bd[:, t, :], dc[:, t, :])
+            turn(unit, 2, ad[:, t, :], dc[:, t, :])
+            sq = work.tile([P, 2, CH], F32, name="sq", bufs=3)
+            nc.scalar.activation(sq[:], unit[:, 0:2, :], ACT.Square)
+            ac_sb = work.tile([P, CH], F32, name="ac_sb", bufs=3)
+            nc.scalar.copy(ac_sb[:], unit[:, 2, :])
+            turn(unit, 3, sq[:, 0, :], sq[:, 1, :])
+            turn(ac, t, ac_sb[:])
+            root = work.tile([P, CH], F32, name="root", bufs=3)
+            nc.scalar.activation(root[:], unit[:, 3, :], ACT.Abs_reciprocal_sqrt, bias=0.5)
+            nc.scalar.activation(inv[:, t, :], root[:], ACT.Square)
+
+        def finish(c):
+            ac, bd, inv = parts[c]
+            num = work.tile([P, PACK, CH], F32, name="num")
+            for t in range(PACK):
+                nc.vector.scalar_tensor_tensor(
+                    num[:, t, :], ac[:, t, :], gs_sb[:, t : t + 1], bd[:, t, :], ALU.mult, ALU.mult
+                )
+            z = work.tile([P, CH, PACK], BF16, name="z", align_bytes=64)
+            nc.vector.tensor_tensor(
+                z[:].rearrange("p (b i) t -> p b t i", i=4),
+                num[:].rearrange("p t (b i) -> p b t i", i=4),
+                inv[:].rearrange("p t (b i) -> p b t i", i=4),
+                ALU.mult,
+            )
+            z_codes = work.tile([P, CH], U32, name="z_codes", align_bytes=64)
+            z_scales = work.tile([P, CH], U8, name="z_scales", align_bytes=64)
+            nc.vector.quantize_mx(
+                out=z_codes[:].bitcast(FP8X4), scales=z_scales[:], in_=z[:].rearrange("p j t -> p (j t)")
+            )
+            score = psum.tile([P, C // P, CH], F32, name=f"score{c}", tag=f"bank{c}")
+            for i in range(C // P):
+                nc.tensor.matmul_mx(
+                    out=score[:, i, :],
+                    lhsT=xc_codes[:, i * P : (i + 1) * P].bitcast(FP8X4),
+                    lhsT_scale=xc_scales[:, i * P : (i + 1) * P],
+                    rhs=z_codes[:].bitcast(FP8X4),
+                    rhs_scale=z_scales[:],
+                    start=True,
+                    stop=True,
+                )
+            res = keep.tile([P, C // P, CH], F32, name=f"res{c}")
+            nc.scalar.mul(res[:], score[:], 0.0625)
+            nc.sync.dma_start(out.rearrange("(i p) j -> p i j", p=P)[:, :, c * CH : (c + 1) * CH], res[:])
+
+        for j0, width in GROUPS:
+            gather(j0, width)
+            for t in range(PACK):
+                for j in range(0, width, CH):
+                    sums((j0 + j) // CH, t)
+        for c in range(S // CH):
+            finish(c)

@@ -19,7 +19,10 @@ ACT = mybir.ActivationFunctionType
 P = 128
 PACK = 4
 CH = 128
-GROUPS = [(0, 256), (256, 128), (384, 128)]
+WINDOW = 2 * S
+TENSOR_PLANES = 2
+LAST_PIECES = [(0, 256), (256, 256)]
+STRETCHES = [(0, 256), (256, 128), (384, 128)]
 W_LOADS = [(0, 256), (256, 256)]
 
 
@@ -40,6 +43,8 @@ def tile_picked_crossrat_none_p_kernel(
         x_bytes = keep.tile([P, T], U8)
         nc.vector.memset(x_bytes[:].bitcast(I32), 0)
 
+        y = [keep.tile([P, WINDOW], F32, name=f"y{t}") for t in range(PACK)]
+        y_neg = [keep.tile([P, WINDOW], F32, name=f"y_neg{t}", tag=f"y_neg{t}") for t in range(PACK)]
         four = keep.tile([P, 1], F32)
         nc.gpsimd.memset(four[:], 4.0)
         warm = keep.tile([P, 1], F32)
@@ -60,16 +65,19 @@ def tile_picked_crossrat_none_p_kernel(
             w_raw.append(raw[:])
         x_packed = keep.tile([P, T], I32)
         nc.sync.dma_start(x_packed[:], x_words[0].rearrange("p n r -> p (n r)").bitcast(I32))
+        q2_sb = load_list(q2, "q2_sb")
         q3_sb = load_list(q3, "q3_sb")
         q0_sb = load_list(q0, "q0_sb")
         q1_sb = load_list(q1, "q1_sb")
-        q2_sb = load_list(q2, "q2_sb")
         for q in range(4):
             rows = slice(32 * q, 32 * q + 4)
             nc.vector.tensor_copy(x_bytes[rows, :].bitcast(I32), staged[rows, :].bitcast(I32))
         gs_sb = keep.tile([P, PACK], F32)
         nc.sync.dma_start(gs_sb[:], gs.rearrange("(p t) o -> p (t o)", t=PACK))
 
+        for t in range(PACK):
+            nc.gpsimd.memset(y[t][:, S:], 0.0)
+            nc.scalar.copy(y_neg[t][:, S:], y[t][:, S:])
         ident = keep.tile([P, P], F32)
         make_identity(nc, ident[:])
 
@@ -109,10 +117,7 @@ def tile_picked_crossrat_none_p_kernel(
             )
         xc_codes = pick_codes(cand_sb, "xc_codes")
 
-        y, y_neg = [], []
         for t in range(PACK):
-            pos = keep.tile([P, S], F32, name=f"y{t}")
-            neg = keep.tile([P, S], F32, name=f"y_neg{t}")
             pieces = [slice(0, 256), slice(256, 512)] if t == 0 else [slice(0, 512)]
             accs = []
             for n, cols in enumerate(pieces):
@@ -129,98 +134,92 @@ def tile_picked_crossrat_none_p_kernel(
                     start=True,
                     stop=True,
                 )
-                nc.scalar.copy(pos[:, cols], acc[:])
+                nc.scalar.copy(y[t][:, cols], acc[:])
                 accs.append(acc)
             for acc, cols in zip(accs, pieces):
-                nc.scalar.mul(neg[:, cols], acc[:], -1.0)
-            y.append(pos)
-            y_neg.append(neg)
+                nc.scalar.mul(y_neg[t][:, cols], acc[:], -1.0)
 
-        def turn(bank, t, *terms):
+        def turn(bank, slot, *terms):
             for n, term in enumerate(terms):
                 nc.tensor.matmul(
-                    bank[:, t, :], term, ident[:], start=(n == 0), stop=(n == len(terms) - 1), is_transpose=True
+                    bank[:, slot, :], term, ident[:], start=(n == 0), stop=(n == len(terms) - 1), is_transpose=True
                 )
 
-        diffs = {}
-
-        def gather(j0, width):
-            cols = slice(j0 // 16, (j0 + width) // 16)
-            d = keep.tile([P, PACK, width], F32, name=f"d{j0}")
-            ad = keep.tile([P, PACK, width], F32, name=f"ad{j0}")
-            bd = keep.tile([P, PACK, width], F32, name=f"bd{j0}")
-            dc = keep.tile([P, PACK, width], F32, name=f"dc{j0}")
-            nc.vector.tensor_copy(d[:, 0, :], y[0][:].indirect(q3_sb[:, cols]))
-            for t in range(PACK):
-                if t + 1 < PACK:
-                    nc.vector.tensor_copy(d[:, t + 1, :], y[t + 1][:].indirect(q3_sb[:, cols]))
-                nc.vector.tensor_tensor(ad[:, t, :], y[t][:].indirect(q0_sb[:, cols]), d[:, t, :], ALU.subtract)
-                nc.vector.tensor_tensor(bd[:, t, :], y[t][:].indirect(q1_sb[:, cols]), d[:, t, :], ALU.subtract)
-                nc.vector.tensor_tensor(dc[:, t, :], y_neg[t][:].indirect(q2_sb[:, cols]), d[:, t, :], ALU.add)
-            for j in range(0, width, CH):
-                diffs[(j0 + j) // CH] = [x[:, :, j : j + CH] for x in (ad, bd, dc)]
-
-        parts = {}
-
-        def sums(c, t):
-            ad, bd, dc = diffs[c]
-            if t == 0:
-                ac = psum.tile([P, PACK, CH], F32, name=f"ac{c}", tag=f"bank{c}")
-                inv = keep.tile([P, PACK, CH], F32, name=f"inv{c}")
-                parts[c] = (ac, bd, inv)
-            ac, bd, inv = parts[c]
-            unit = psum.tile([P, 4, CH], F32, name="unit", tag="unit", bufs=4)
-            turn(unit, 0, ad[:, t, :])
-            turn(unit, 1, bd[:, t, :], dc[:, t, :])
-            turn(unit, 2, ad[:, t, :], dc[:, t, :])
-            sq = work.tile([P, 2, CH], F32, name="sq", bufs=3)
-            nc.scalar.activation(sq[:], unit[:, 0:2, :], ACT.Square)
-            ac_sb = work.tile([P, CH], F32, name="ac_sb", bufs=3)
-            nc.scalar.copy(ac_sb[:], unit[:, 2, :])
-            turn(unit, 3, sq[:, 0, :], sq[:, 1, :])
-            turn(ac, t, ac_sb[:])
-            root = work.tile([P, CH], F32, name="root", bufs=3)
-            nc.scalar.activation(root[:], unit[:, 3, :], ACT.Abs_reciprocal_sqrt, bias=0.5)
-            nc.scalar.activation(inv[:, t, :], root[:], ACT.Square)
-
-        def finish(c):
-            ac, bd, inv = parts[c]
-            num = work.tile([P, PACK, CH], F32, name="num")
-            for t in range(PACK):
-                nc.vector.scalar_tensor_tensor(
-                    num[:, t, :], ac[:, t, :], gs_sb[:, t : t + 1], bd[:, t, :], ALU.mult, ALU.mult
+        inv = keep.tile([P, PACK, S], F32)
+        ac = [keep.tile([P, S], F32, name=f"ac{t}") for t in range(PACK)]
+        db = [keep.tile([P, S], F32, name=f"db{t}") for t in range(PACK)]
+        for t in range(PACK):
+            c_pos = keep.tile([P, S], F32, name=f"c_pos{t}")
+            d_neg = keep.tile([P, S], F32, name=f"d_neg{t}")
+            if t < TENSOR_PLANES:
+                c_minus_d = [c_pos, d_neg]
+            else:
+                cd = keep.tile([P, S], F32, name=f"cd{t}")
+                c_minus_d = [cd]
+            for j0, width in LAST_PIECES if t == PACK - 1 else [(0, S)]:
+                cols = slice(j0, j0 + width)
+                entries = slice(j0 // 16, (j0 + width) // 16)
+                nc.vector.tensor_copy(c_pos[:, cols], y[t][:].indirect(q2_sb[:, entries]))
+                nc.vector.tensor_copy(d_neg[:, cols], y_neg[t][:].indirect(q3_sb[:, entries]))
+                nc.vector.tensor_tensor(
+                    ac[t][:, cols], y[t][:].indirect(q0_sb[:, entries]), c_pos[:, cols], ALU.subtract
                 )
-            z = work.tile([P, CH, PACK], BF16, name="z", align_bytes=64)
+                if t >= TENSOR_PLANES:
+                    nc.vector.tensor_tensor(cd[:, cols], c_pos[:, cols], d_neg[:, cols], ALU.add)
+                nc.vector.tensor_tensor(
+                    db[t][:, cols], y_neg[t][:].indirect(q1_sb[:, entries]), d_neg[:, cols], ALU.subtract
+                )
+                for j in range(j0, j0 + width, CH):
+                    part = slice(j, j + CH)
+                    unit = psum.tile([P, 3, CH], F32, name="unit", tag="unit", bufs=4)
+                    turn(unit, 0, *[term[:, part] for term in c_minus_d + [ac[t]]])
+                    turn(unit, 1, *[term[:, part] for term in c_minus_d + [db[t]]])
+                    sq = work.tile([P, 2, CH], F32, name="sq", bufs=3)
+                    nc.scalar.activation(sq[:], unit[:, 0:2, :], ACT.Square)
+                    turn(unit, 2, sq[:, 0, :], sq[:, 1, :])
+                    root = work.tile([P, CH], F32, name="root", bufs=3)
+                    nc.scalar.activation(root[:], unit[:, 2, :], ACT.Abs_reciprocal_sqrt, bias=0.5)
+                    nc.scalar.activation(inv[:, t, part], root[:], ACT.Square)
+
+        num = keep.tile([P, PACK, S], F32, tag=f"y_neg{PACK - 1}")
+        for t in range(PACK):
+            nc.vector.scalar_tensor_tensor(
+                num[:, t, :], ac[t][:], gs_sb[:, t : t + 1], db[t][:], ALU.mult, ALU.mult
+            )
+
+        out_rows = out.rearrange("(i p) j -> p i j", p=P)
+        banks = [["bank0", "bank1"], ["bank2"], ["bank3", "bank0"]]
+        for (j0, width), tags in zip(STRETCHES, banks):
+            cols = slice(j0, j0 + width)
+            z = keep.tile([P, width, PACK], BF16, name=f"z{j0}", align_bytes=64)
             nc.vector.tensor_tensor(
                 z[:].rearrange("p (b i) t -> p b t i", i=4),
-                num[:].rearrange("p t (b i) -> p b t i", i=4),
-                inv[:].rearrange("p t (b i) -> p b t i", i=4),
+                num[:, :, cols].rearrange("p t (b i) -> p b t i", i=4),
+                inv[:, :, cols].rearrange("p t (b i) -> p b t i", i=4),
                 ALU.mult,
             )
-            z_codes = work.tile([P, CH], U32, name="z_codes", align_bytes=64)
-            z_scales = work.tile([P, CH], U8, name="z_scales", align_bytes=64)
+            z_codes = keep.tile([P, width], U32, name=f"z_codes{j0}", align_bytes=64)
+            z_scales = keep.tile([P, width], U8, name=f"z_scales{j0}", align_bytes=64)
             nc.vector.quantize_mx(
                 out=z_codes[:].bitcast(FP8X4), scales=z_scales[:], in_=z[:].rearrange("p j t -> p (j t)")
             )
-            score = psum.tile([P, C // P, CH], F32, name=f"score{c}", tag=f"bank{c}")
-            for i in range(C // P):
-                nc.tensor.matmul_mx(
-                    out=score[:, i, :],
-                    lhsT=xc_codes[:, i * P : (i + 1) * P].bitcast(FP8X4),
-                    lhsT_scale=xc_scales[:, i * P : (i + 1) * P],
-                    rhs=z_codes[:].bitcast(FP8X4),
-                    rhs_scale=z_scales[:],
-                    start=True,
-                    stop=True,
-                )
-            res = keep.tile([P, C // P, CH], F32, name=f"res{c}")
-            nc.scalar.mul(res[:], score[:], 0.0625)
-            nc.sync.dma_start(out.rearrange("(i p) j -> p i j", p=P)[:, :, c * CH : (c + 1) * CH], res[:])
-
-        for j0, width in GROUPS:
-            gather(j0, width)
-            for t in range(PACK):
-                for j in range(0, width, CH):
-                    sums((j0 + j) // CH, t)
-        for c in range(S // CH):
-            finish(c)
+            rows = C // P // len(tags)
+            for n, tag in enumerate(tags):
+                score = psum.tile([P, rows, width], F32, name=f"score{j0}_{n}", tag=tag)
+                for i in range(rows):
+                    picked = slice((n * rows + i) * P, (n * rows + i + 1) * P)
+                    nc.tensor.matmul_mx(
+                        out=score[:, i, :],
+                        lhsT=xc_codes[:, picked].bitcast(FP8X4),
+                        lhsT_scale=xc_scales[:, picked],
+                        rhs=z_codes[:].bitcast(FP8X4),
+                        rhs_scale=z_scales[:],
+                        start=True,
+                        stop=True,
+                    )
+                res = keep.tile([P, rows, width], F32, name=f"res{j0}_{n}")
+                if j0 + width == S and n == 1:
+                    nc.vector.tensor_scalar_mul(res[:], score[:], -0.0625)
+                else:
+                    nc.scalar.mul(res[:], score[:], -0.0625)
+                nc.sync.dma_start(out_rows[:, n * rows : (n + 1) * rows, cols], res[:])

@@ -21,7 +21,7 @@ PACK = 4
 CH = 128
 WINDOW = 2 * S
 TENSOR_PLANES = 2
-LAST_PIECES = [(0, 256), (256, 256)]
+HALVES = [(0, 256), (256, 256)]
 STRETCHES = [(0, 256), (256, 128), (384, 128)]
 W_LOADS = [(0, 256), (256, 256)]
 
@@ -156,7 +156,7 @@ def tile_picked_crossrat_none_p_kernel(
             else:
                 cd = keep.tile([P, S], F32, name=f"cd{t}")
                 c_minus_d = [cd]
-            for j0, width in LAST_PIECES if t == PACK - 1 else [(0, S)]:
+            for j0, width in HALVES if t in (0, PACK - 1) else [(0, S)]:
                 cols = slice(j0, j0 + width)
                 entries = slice(j0 // 16, (j0 + width) // 16)
                 nc.vector.tensor_copy(c_pos[:, cols], y[t][:].indirect(q2_sb[:, entries]))
@@ -169,10 +169,11 @@ def tile_picked_crossrat_none_p_kernel(
                 nc.vector.tensor_tensor(
                     db[t][:, cols], y_neg[t][:].indirect(q1_sb[:, entries]), d_neg[:, cols], ALU.subtract
                 )
-                for j in range(j0, j0 + width, CH):
-                    part = slice(j, j + CH)
-                    unit = psum.tile([P, 3, CH], F32, name="unit", tag="unit", bufs=4)
+                parts = [slice(j, j + CH) for j in range(j0, j0 + width, CH)]
+                units = [psum.tile([P, 3, CH], F32, name="unit", tag="unit", bufs=4) for part in parts]
+                for unit, part in zip(units, parts):
                     turn(unit, 0, *[term[:, part] for term in c_minus_d + [ac[t]]])
+                for unit, part in zip(units, parts):
                     turn(unit, 1, *[term[:, part] for term in c_minus_d + [db[t]]])
                     sq = work.tile([P, 2, CH], F32, name="sq", bufs=3)
                     nc.scalar.activation(sq[:], unit[:, 0:2, :], ACT.Square)

from contextlib import ExitStack

import concourse.mybir as mybir
from concourse.masks import make_identity

K, T, S, H, C = 512, 2048, 512, 512, 512
FLOPS = 2 * K * H * S + 2 * K * C * S

F32 = mybir.dt.float32
BF16 = mybir.dt.bfloat16
I32 = mybir.dt.int32
U32 = mybir.dt.uint32
U16 = mybir.dt.uint16
U8 = mybir.dt.uint8
FP8X4 = mybir.dt.float8_e4m3fn_x4
ALU = mybir.AluOpType
ACT = mybir.ActivationFunctionType

P = 128
PACK = 4
CH = 128
WINDOW = 2 * S
TENSOR_PLANES = 2
HALVES = [(0, 256), (256, 256)]
STRETCHES = [(0, 256), (256, 128), (384, 128)]
W_LOADS = [(0, 256), (256, 256)]


def tile_picked_crossrat_none_p_kernel(
    tc, x_words, x_scales, w1, gs, offs, q0, q1, q2, q3, cand, out
):
    nc = tc.nc
    with ExitStack() as ctx:
        keep = ctx.enter_context(tc.tile_pool(name="keep", bufs=1))
        work = ctx.enter_context(tc.tile_pool(name="work", bufs=2))
        psum = ctx.enter_context(tc.psum_pool(name="psum", bufs=1))

        def load_list(src, name):
            lst = keep.tile([P, S // 16], U16, name=name)
            nc.sync.dma_start(lst[:], src)
            return lst

        x_bytes = keep.tile([P, T], U8)
        nc.vector.memset(x_bytes[:].bitcast(I32), 0)

        y = [keep.tile([P, WINDOW], F32, name=f"y{t}") for t in range(PACK)]
        y_neg = [keep.tile([P, WINDOW], F32, name=f"y_neg{t}", tag=f"y_neg{t}") for t in range(PACK)]
        four = keep.tile([P, 1], F32)
        nc.gpsimd.memset(four[:], 4.0)
        warm = keep.tile([P, 1], F32)
        nc.scalar.activation(warm[:], four[:], ACT.Abs_reciprocal_sqrt)

        staged = keep.tile([P, T], U8)
        for q in range(4):
            nc.sync.dma_start(
                staged[32 * q : 32 * q + 4, :].bitcast(I32), x_scales[0, 4 * q : 4 * q + 4, :].bitcast(I32)
            )
        offs_sb = load_list(offs, "offs_sb")
        cand_sb = load_list(cand, "cand_sb")
        w_rows = w1.rearrange("(p j) c -> p j c", j=PACK)
        w_raw = []
        for n, (c0, cw) in enumerate(W_LOADS):
            raw = keep.tile([P, PACK, cw], F32, name=f"w_raw{n}")
            nc.sync.dma_start(raw[:], w_rows[:, :, c0 : c0 + cw])
            w_raw.append(raw[:])
        x_packed = keep.tile([P, T], I32)
        nc.sync.dma_start(x_packed[:], x_words[0].rearrange("p n r -> p (n r)").bitcast(I32))
        q2_sb = load_list(q2, "q2_sb")
        q3_sb = load_list(q3, "q3_sb")
        q0_sb = load_list(q0, "q0_sb")
        q1_sb = load_list(q1, "q1_sb")
        for q in range(4):
            rows = slice(32 * q, 32 * q + 4)
            nc.vector.tensor_copy(x_bytes[rows, :].bitcast(I32), staged[rows, :].bitcast(I32))
        gs_sb = keep.tile([P, PACK], F32)
        nc.sync.dma_start(gs_sb[:], gs.rearrange("(p t) o -> p (t o)", t=PACK))

        for t in range(PACK):
            nc.gpsimd.memset(y[t][:, S:], 0.0)
            nc.scalar.copy(y_neg[t][:, S:], y[t][:, S:])
        ident = keep.tile([P, P], F32)
        make_identity(nc, ident[:])

        def pick_scales(lst, name):
            scales = keep.tile([P, S], U8, name=name, align_bytes=64)
            nc.vector.tensor_copy(scales[:], x_bytes[:].indirect(lst[:]))
            return scales

        def pick_codes(lst, name):
            codes = keep.tile([P, S], U32, name=name, align_bytes=64)
            nc.vector.tensor_copy(codes[:], x_packed[:].bitcast(U32).indirect(lst[:]))
            return codes

        xq_scales = pick_scales(offs_sb, "xq_scales")
        xc_scales = pick_scales(cand_sb, "xc_scales")

        w_half = [keep.tile([P, PACK, 64, PACK], BF16, name=f"w_half{h}", tag=f"w_half{h}", align_bytes=64) for h in range(2)]
        w_codes = keep.tile([P, PACK, P], U32, align_bytes=64)
        w_scales = keep.tile([P, PACK, P], U8, align_bytes=64)
        for n, (c0, cw) in enumerate(W_LOADS):
            h, m0 = divmod(c0 // PACK, 64)
            dst = w_half[h][:, :, m0 : m0 + cw // PACK, :].rearrange("p t m j -> p m j t")
            src = w_raw[n].rearrange("p j (m t) -> p m j t", t=PACK)
            nc.scalar.copy(dst, src)
        for h in range(2):
            for t in range(PACK):
                nc.vector.quantize_mx(
                    out=w_codes[:, t, 64 * h : 64 * h + 64].bitcast(FP8X4),
                    scales=w_scales[:, t, 64 * h : 64 * h + 64],
                    in_=w_half[h][:, t, :, :].rearrange("p m j -> p (m j)"),
                )

        xq_codes = keep.tile([P, S], U32, align_bytes=64)
        for h in range(2):
            nc.vector.tensor_copy(
                xq_codes[:, 256 * h : 256 * h + 256], x_packed[:].bitcast(U32).indirect(offs_sb[:, 16 * h : 16 * h + 16])
            )
        xc_codes = pick_codes(cand_sb, "xc_codes")

        for t in range(PACK):
            pieces = [slice(0, 256), slice(256, 512)] if t == 0 else [slice(0, 512)]
            accs = []
            for n, cols in enumerate(pieces):
                if n == 0:
                    acc = psum.tile([P, cols.stop - cols.start], F32, name=f"y_acc{t}", tag=f"bank{t}")
                else:
                    acc = psum.tile([P, cols.stop - cols.start], F32, name="y_late", tag="unit", bufs=4)
                nc.tensor.matmul_mx(
                    out=acc[:],
                    lhsT=w_codes[:, t, :].bitcast(FP8X4),
                    lhsT_scale=w_scales[:, t, :],
                    rhs=xq_codes[:, cols].bitcast(FP8X4),
                    rhs_scale=xq_scales[:, cols],
                    start=True,
                    stop=True,
                )
                nc.scalar.copy(y[t][:, cols], acc[:])
                accs.append(acc)
            for acc, cols in zip(accs, pieces):
                nc.scalar.mul(y_neg[t][:, cols], acc[:], -1.0)

        def turn(bank, slot, *terms):
            for n, term in enumerate(terms):
                nc.tensor.matmul(
                    bank[:, slot, :], term, ident[:], start=(n == 0), stop=(n == len(terms) - 1), is_transpose=True
                )

        inv = keep.tile([P, PACK, S], F32)
        ac = [keep.tile([P, S], F32, name=f"ac{t}") for t in range(PACK)]
        db = [keep.tile([P, S], F32, name=f"db{t}") for t in range(PACK)]
        for t in range(PACK):
            c_pos = keep.tile([P, S], F32, name=f"c_pos{t}")
            d_neg = keep.tile([P, S], F32, name=f"d_neg{t}")
            if t < TENSOR_PLANES:
                c_minus_d = [c_pos, d_neg]
            else:
                cd = keep.tile([P, S], F32, name=f"cd{t}")
                c_minus_d = [cd]
            for j0, width in HALVES if t in (0, PACK - 1) else [(0, S)]:
                cols = slice(j0, j0 + width)
                entries = slice(j0 // 16, (j0 + width) // 16)
                nc.vector.tensor_copy(c_pos[:, cols], y[t][:].indirect(q2_sb[:, entries]))
                nc.vector.tensor_copy(d_neg[:, cols], y_neg[t][:].indirect(q3_sb[:, entries]))
                nc.vector.tensor_tensor(
                    ac[t][:, cols], y[t][:].indirect(q0_sb[:, entries]), c_pos[:, cols], ALU.subtract
                )
                if t >= TENSOR_PLANES:
                    nc.vector.tensor_tensor(cd[:, cols], c_pos[:, cols], d_neg[:, cols], ALU.add)
                nc.vector.tensor_tensor(
                    db[t][:, cols], y_neg[t][:].indirect(q1_sb[:, entries]), d_neg[:, cols], ALU.subtract
                )
                parts = [slice(j, j + CH) for j in range(j0, j0 + width, CH)]
                units = [psum.tile([P, 3, CH], F32, name="unit", tag="unit", bufs=4) for part in parts]
                for unit, part in zip(units, parts):
                    turn(unit, 0, *[term[:, part] for term in c_minus_d + [ac[t]]])
                for unit, part in zip(units, parts):
                    turn(unit, 1, *[term[:, part] for term in c_minus_d + [db[t]]])
                    sq = work.tile([P, 2, CH], F32, name="sq", bufs=3)
                    nc.scalar.activation(sq[:], unit[:, 0:2, :], ACT.Square)
                    turn(unit, 2, sq[:, 0, :], sq[:, 1, :])
                    root = work.tile([P, CH], F32, name="root", bufs=3)
                    nc.scalar.activation(root[:], unit[:, 2, :], ACT.Abs_reciprocal_sqrt, bias=0.5)
                    nc.scalar.activation(inv[:, t, part], root[:], ACT.Square)

        num = keep.tile([P, PACK, S], F32, tag=f"y_neg{PACK - 1}")
        for t in range(PACK):
            nc.vector.scalar_tensor_tensor(
                num[:, t, :], ac[t][:], gs_sb[:, t : t + 1], db[t][:], ALU.mult, ALU.mult
            )

        out_rows = out.rearrange("(i p) j -> p i j", p=P)
        banks = [["bank0", "bank1"], ["bank2"], ["bank3", "bank0"]]
        for (j0, width), tags in zip(STRETCHES, banks):
            cols = slice(j0, j0 + width)
            z = keep.tile([P, width, PACK], BF16, name=f"z{j0}", align_bytes=64)
            nc.vector.tensor_tensor(
                z[:].rearrange("p (b i) t -> p b t i", i=4),
                num[:, :, cols].rearrange("p t (b i) -> p b t i", i=4),
                inv[:, :, cols].rearrange("p t (b i) -> p b t i", i=4),
                ALU.mult,
            )
            z_codes = keep.tile([P, width], U32, name=f"z_codes{j0}", align_bytes=64)
            z_scales = keep.tile([P, width], U8, name=f"z_scales{j0}", align_bytes=64)
            nc.vector.quantize_mx(
                out=z_codes[:].bitcast(FP8X4), scales=z_scales[:], in_=z[:].rearrange("p j t -> p (j t)")
            )
            rows = C // P // len(tags)
            for n, tag in enumerate(tags):
                score = psum.tile([P, rows, width], F32, name=f"score{j0}_{n}", tag=tag)
                for i in range(rows):
                    picked = slice((n * rows + i) * P, (n * rows + i + 1) * P)
                    nc.tensor.matmul_mx(
                        out=score[:, i, :],
                        lhsT=xc_codes[:, picked].bitcast(FP8X4),
                        lhsT_scale=xc_scales[:, picked],
                        rhs=z_codes[:].bitcast(FP8X4),
                        rhs_scale=z_scales[:],
                        start=True,
                        stop=True,
                    )
                res = keep.tile([P, rows, width], F32, name=f"res{j0}_{n}")
                if j0 + width == S and n == 1:
                    nc.vector.tensor_scalar_mul(res[:], score[:], -0.0625)
                else:
                    nc.scalar.mul(res[:], score[:], -0.0625)
                nc.sync.dma_start(out_rows[:, n * rows : (n + 1) * rows, cols], res[:])
